import numpy as np
CORES = [6,10,22,26,38,42,54,58]
N = 8
def setup_inputs(rng):
    return {"x": rng.standard_normal((N, 128, 1024), dtype=np.float32)}
def reference(x):
    g = np.concatenate(list(x), axis=1)
    return {"y": np.broadcast_to(g, (N,) + g.shape)}

@@ -1,0 +1,142 @@
+from concourse.bass import DstId, RemoteDMATransfer
+
+CORES = [6, 10, 22, 26, 38, 42, 54, 58]
+ROWS = [16, 16, 32]
+MODE = "QQP"
+OWN = "g"
+C = len(ROWS)
+BASE = [2 * sum(ROWS[:k]) for k in range(C)]
+LO, HI = 0x00FF, 0xFF00
+
+
+def roles(chip):
+    b = chip * 8
+    if chip % 2 == 0:
+        return b + 6, 0, {0: (b + 4, b + 7), 1: (b + 2, b + 3)}
+    return b + 2, 1, {1: (b + 0, b + 3), 0: (b + 6, b + 7)}
+
+
+def bits(m):
+    return bin(m).count("1")
+
+
+def slot(j, k, d):
+    return k * 16 + j * 2 + d
+
+
+def build():
+    ops, sent, arr = {}, {}, {}
+
+    def qu(core, name):
+        return ops.setdefault(core, {"g": [], "sync": [], "scalar": []})[name]
+
+    def rd(core, transfers):
+        for s, m, dsts in transfers:
+            for d in dsts:
+                arr[(d, s)] = bits(m)
+            sent[core] = sent.get(core, 0) + bits(m)
+        qu(core, "g").append(("rd", transfers))
+
+    def wait_arr(core, name, s):
+        qu(core, name).append(("wait", "a%d" % s, arr[(core, s)]))
+
+    for j in range(8):
+        rk, rdie, hs = roles(j)
+        for k in range(C):
+            s = slot(j, k, 0)
+            qu(rk, ("sync", "scalar")[k % 2]).append(("ld", s, s + 2, "a%d" % s))
+            qu(rk, "g").append(("wait", "a%d" % s, 16))
+            if MODE[k] == "Q":
+                rd(rk, [(s + d, (LO, HI)[d], [hs[d][0], hs[d][1]]) for d in (0, 1)])
+            else:
+                rd(rk, [(s + d, (LO, HI)[d], [hs[d][0]]) for d in (0, 1)])
+        if OWN != "g":
+            qu(rk, "g").append(("inc", "ho", 1))
+            qu(rk, OWN).append(("wait", "ho", 1))
+        qu(rk, OWN).append(("own", j, "own"))
+    for j in range(8):
+        rk, rdie, hs = roles(j)
+        for d in (0, 1):
+            S, F = hs[d]
+            for k in range(C):
+                s = slot(j, k, d)
+                wait_arr(S, "g", s)
+                if MODE[k] == "Q":
+                    rd(S, [(s, LO, [roles((j + 2 * i) % 8)[0] for i in (1, 2, 3)])])
+                    continue
+                far = [roles((j + 2 * i) % 8)[2][d][1] for i in (1, 2, 3)]
+                if d != rdie:
+                    rd(S, [(s, LO, [roles(j ^ 1)[0]] + far)])
+                else:
+                    rd(S, [(s, LO, far), (s, HI, [F])])
+    for c in range(8):
+        rk, rdie, hs = roles(c)
+        mate = roles(c ^ 1)[0]
+        for d in (0, 1):
+            F = hs[d][1]
+            for k in range(C):
+                if MODE[k] == "Q":
+                    s = slot(c, k, d)
+                    wait_arr(F, "g", s)
+                    rd(F, [(s, LO, [roles(((c ^ 1) + 2 * i) % 8)[0] for i in (0, 1, 2, 3)])])
+                    continue
+                if d == rdie:
+                    s = slot(c, k, d)
+                    wait_arr(F, "g", s)
+                    rd(F, [(s, LO, [mate])])
+                for i in (1, 2, 3):
+                    s = slot((c - 2 * i) % 8, k, d)
+                    wait_arr(F, "g", s)
+                    rd(F, [(s, LO, [mate]), (s, HI, [rk])])
+    for c in range(8):
+        rk = roles(c)[0]
+        plan = {"sync": [((c - 2 * i) % 8, k) for k in range(C) for i in (1, 2, 3)],
+                "scalar": [(((c ^ 1) - 2 * i) % 8, k) for k in range(C) for i in (1, 2, 3)],
+                "g": [(c ^ 1, k) for k in range(C)]}
+        for name in ("g", "sync", "scalar"):
+            for src, k in plan[name]:
+                s = slot(src, k, 0)
+                wait_arr(rk, name, s)
+                wait_arr(rk, name, s + 1)
+                qu(rk, name).append(("st", s, s + 2, "st_" + name))
+            qu(rk, name).append(("wait", "st_" + name, 16 * len(plan[name])))
+        qu(rk, OWN).append(("wait", "own", 16))
+    for core in sent:
+        qu(core, "g").append(("wait", "sent", sent[core]))
+    return ops
+
+
+PLAN = build()
+SCRATCH = dict(("L%d" % k, ("dram", [16, 128, 8 * ROWS[k]], "float32")) for k in range(C))
+SEMAPHORES = ["sent", "own", "ho", "st_g", "st_sync", "st_scalar"] + ["a%d" % i for i in range(16 * C)]
+
+
+def rank_program(g, core, T, topo):
+    prog = PLAN.get(core)
+    if prog is None:
+        return
+    for name, q in (("g", g), ("sync", g.sync), ("scalar", g.scalar)):
+        for o in prog[name]:
+            if o[0] == "wait":
+                q.wait_ge(T.sem[o[1]], o[2])
+            elif o[0] == "inc":
+                q.sem_inc(T.sem[o[1]], o[2])
+            elif o[0] == "ld" or o[0] == "st":
+                k, a, b = o[1] // 16, o[1] % 16, o[1] % 16 + o[2] - o[1]
+                j = a // 2
+                r0 = BASE[k] + (a % 2) * ROWS[k]
+                r1 = r0 + (b - a) * ROWS[k]
+                if o[0] == "ld":
+                    q.dma_start(T["L%d" % k][a:b], T.x[r0:r1, :]).then_inc(T.sem[o[3]], 16)
+                else:
+                    q.dma_start(T.y[r0:r1, 1024 * j:1024 * (j + 1)], T["L%d" % k][a:b]).then_inc(T.sem[o[3]], 16)
+            elif o[0] == "own":
+                q.dma_start(T.y[:, 1024 * o[1]:1024 * (o[1] + 1)], T.x[:, :]).then_inc(T.sem[o[2]], 16)
+            else:
+                trs = []
+                for s, m, dsts in o[1]:
+                    ap = T["L%d" % (s // 16)][s % 16]
+                    ids = [DstId(rid=topo.addr(d)[0], pnc=topo.addr(d)[1]) for d in dsts]
+                    trs.append(RemoteDMATransfer(dst_ids=ids, dma_engine_mask=m, remote_sem=T.sem["a%d" % s],
+                                                 srcs=[ap], dsts=[ap for d in dsts]))
+                q.remote_dma_fused(trs, local_sem=T.sem.sent)

@@ -2,11 +2,12 @@ from concourse.bass import DstId, RemoteDMATransfer
 
 CORES = [6, 10, 22, 26, 38, 42, 54, 58]
 ROWS = [16, 16, 32]
-MODE = "QQP"
-OWN = "g"
+MODE = "PPP"
+BATCH = False
 C = len(ROWS)
 BASE = [2 * sum(ROWS[:k]) for k in range(C)]
 LO, HI = 0x00FF, 0xFF00
+SPLIT = {1: (0xFF,), 3: (0x0F, 0x30, 0xC0), 4: (0x03, 0x0C, 0x30, 0xC0)}
 
 
 def roles(chip):
@@ -40,20 +41,21 @@ def build():
     def wait_arr(core, name, s):
         qu(core, name).append(("wait", "a%d" % s, arr[(core, s)]))
 
+    def ranks(c):
+        return [roles((c + 2 * i) % 8)[0] for i in (1, 2, 3)]
+
     for j in range(8):
         rk, rdie, hs = roles(j)
         for k in range(C):
             s = slot(j, k, 0)
             qu(rk, ("sync", "scalar")[k % 2]).append(("ld", s, s + 2, "a%d" % s))
             qu(rk, "g").append(("wait", "a%d" % s, 16))
-            if MODE[k] == "Q":
-                rd(rk, [(s + d, (LO, HI)[d], [hs[d][0], hs[d][1]]) for d in (0, 1)])
+            if MODE[k] == "M":
+                rd(rk, [(s, 0x0F00, [hs[0][0]]), (s + 1, 0xF000, [hs[1][0]]),
+                        (s + rdie, LO, [roles(j ^ 1)[2][rdie][1]])])
             else:
                 rd(rk, [(s + d, (LO, HI)[d], [hs[d][0]]) for d in (0, 1)])
-        if OWN != "g":
-            qu(rk, "g").append(("inc", "ho", 1))
-            qu(rk, OWN).append(("wait", "ho", 1))
-        qu(rk, OWN).append(("own", j, "own"))
+        qu(rk, "g").append(("own", j, "own"))
     for j in range(8):
         rk, rdie, hs = roles(j)
         for d in (0, 1):
@@ -61,8 +63,8 @@ def build():
             for k in range(C):
                 s = slot(j, k, d)
                 wait_arr(S, "g", s)
-                if MODE[k] == "Q":
-                    rd(S, [(s, LO, [roles((j + 2 * i) % 8)[0] for i in (1, 2, 3)])])
+                if MODE[k] == "M":
+                    rd(S, [(s, LO, ([] if d == rdie else [roles(j ^ 1)[2][d][1]]) + ranks(j))])
                     continue
                 far = [roles((j + 2 * i) % 8)[2][d][1] for i in (1, 2, 3)]
                 if d != rdie:
@@ -75,19 +77,22 @@ def build():
         for d in (0, 1):
             F = hs[d][1]
             for k in range(C):
-                if MODE[k] == "Q":
-                    s = slot(c, k, d)
+                if MODE[k] == "M":
+                    s = slot(c ^ 1, k, d)
                     wait_arr(F, "g", s)
-                    rd(F, [(s, LO, [roles(((c ^ 1) + 2 * i) % 8)[0] for i in (0, 1, 2, 3)])])
+                    rd(F, [(s, LO, ranks(c)), (s, HI, [rk])])
                     continue
-                if d == rdie:
-                    s = slot(c, k, d)
+                far = [slot((c - 2 * i) % 8, k, d) for i in (1, 2, 3)]
+                out = ([slot(c, k, d)] if d == rdie else []) + far
+                if BATCH:
+                    for s in out:
+                        wait_arr(F, "g", s)
+                    rd(F, [(s, SPLIT[len(out)][n], [mate]) for n, s in enumerate(out)]
+                       + [(s, SPLIT[3][n] << 8, [rk]) for n, s in enumerate(far)])
+                    continue
+                for s in out:
                     wait_arr(F, "g", s)
-                    rd(F, [(s, LO, [mate])])
-                for i in (1, 2, 3):
-                    s = slot((c - 2 * i) % 8, k, d)
-                    wait_arr(F, "g", s)
-                    rd(F, [(s, LO, [mate]), (s, HI, [rk])])
+                    rd(F, [(s, LO, [mate])] + ([(s, HI, [rk])] if s in far else []))
     for c in range(8):
         rk = roles(c)[0]
         plan = {"sync": [((c - 2 * i) % 8, k) for k in range(C) for i in (1, 2, 3)],
@@ -100,7 +105,7 @@ def build():
                 wait_arr(rk, name, s + 1)
                 qu(rk, name).append(("st", s, s + 2, "st_" + name))
             qu(rk, name).append(("wait", "st_" + name, 16 * len(plan[name])))
-        qu(rk, OWN).append(("wait", "own", 16))
+        qu(rk, "g").append(("wait", "own", 16))
     for core in sent:
         qu(core, "g").append(("wait", "sent", sent[core]))
     return ops
@@ -108,7 +113,7 @@ def build():
 
 PLAN = build()
 SCRATCH = dict(("L%d" % k, ("dram", [16, 128, 8 * ROWS[k]], "float32")) for k in range(C))
-SEMAPHORES = ["sent", "own", "ho", "st_g", "st_sync", "st_scalar"] + ["a%d" % i for i in range(16 * C)]
+SEMAPHORES = ["sent", "own", "st_g", "st_sync", "st_scalar"] + ["a%d" % i for i in range(16 * C)]
 
 
 def rank_program(g, core, T, topo):
@@ -119,8 +124,6 @@ def rank_program(g, core, T, topo):
         for o in prog[name]:
             if o[0] == "wait":
                 q.wait_ge(T.sem[o[1]], o[2])
-            elif o[0] == "inc":
-                q.sem_inc(T.sem[o[1]], o[2])
             elif o[0] == "ld" or o[0] == "st":
                 k, a, b = o[1] // 16, o[1] % 16, o[1] % 16 + o[2] - o[1]
                 j = a // 2

@@ -1,8 +1,8 @@
 from concourse.bass import DstId, RemoteDMATransfer
 
 CORES = [6, 10, 22, 26, 38, 42, 54, 58]
-ROWS = [16, 16, 32]
-MODE = "PPP"
+ROWS = [8, 16, 24, 16]
+MODE = "PPPP"
 BATCH = False
 C = len(ROWS)
 BASE = [2 * sum(ROWS[:k]) for k in range(C)]

from concourse.bass import DstId, RemoteDMATransfer

CORES = [6, 10, 22, 26, 38, 42, 54, 58]
ROWS = [8, 16, 24, 16]
MODE = "PPPP"
BATCH = False
C = len(ROWS)
BASE = [2 * sum(ROWS[:k]) for k in range(C)]
LO, HI = 0x00FF, 0xFF00
SPLIT = {1: (0xFF,), 3: (0x0F, 0x30, 0xC0), 4: (0x03, 0x0C, 0x30, 0xC0)}


def roles(chip):
    b = chip * 8
    if chip % 2 == 0:
        return b + 6, 0, {0: (b + 4, b + 7), 1: (b + 2, b + 3)}
    return b + 2, 1, {1: (b + 0, b + 3), 0: (b + 6, b + 7)}


def bits(m):
    return bin(m).count("1")


def slot(j, k, d):
    return k * 16 + j * 2 + d


def build():
    ops, sent, arr = {}, {}, {}

    def qu(core, name):
        return ops.setdefault(core, {"g": [], "sync": [], "scalar": []})[name]

    def rd(core, transfers):
        for s, m, dsts in transfers:
            for d in dsts:
                arr[(d, s)] = bits(m)
            sent[core] = sent.get(core, 0) + bits(m)
        qu(core, "g").append(("rd", transfers))

    def wait_arr(core, name, s):
        qu(core, name).append(("wait", "a%d" % s, arr[(core, s)]))

    def ranks(c):
        return [roles((c + 2 * i) % 8)[0] for i in (1, 2, 3)]

    for j in range(8):
        rk, rdie, hs = roles(j)
        for k in range(C):
            s = slot(j, k, 0)
            qu(rk, ("sync", "scalar")[k % 2]).append(("ld", s, s + 2, "a%d" % s))
            qu(rk, "g").append(("wait", "a%d" % s, 16))
            if MODE[k] == "M":
                rd(rk, [(s, 0x0F00, [hs[0][0]]), (s + 1, 0xF000, [hs[1][0]]),
                        (s + rdie, LO, [roles(j ^ 1)[2][rdie][1]])])
            else:
                rd(rk, [(s + d, (LO, HI)[d], [hs[d][0]]) for d in (0, 1)])
        qu(rk, "g").append(("own", j, "own"))
    for j in range(8):
        rk, rdie, hs = roles(j)
        for d in (0, 1):
            S, F = hs[d]
            for k in range(C):
                s = slot(j, k, d)
                wait_arr(S, "g", s)
                if MODE[k] == "M":
                    rd(S, [(s, LO, ([] if d == rdie else [roles(j ^ 1)[2][d][1]]) + ranks(j))])
                    continue
                far = [roles((j + 2 * i) % 8)[2][d][1] for i in (1, 2, 3)]
                if d != rdie:
                    rd(S, [(s, LO, [roles(j ^ 1)[0]] + far)])
                else:
                    rd(S, [(s, LO, far), (s, HI, [F])])
    for c in range(8):
        rk, rdie, hs = roles(c)
        mate = roles(c ^ 1)[0]
        for d in (0, 1):
            F = hs[d][1]
            for k in range(C):
                if MODE[k] == "M":
                    s = slot(c ^ 1, k, d)
                    wait_arr(F, "g", s)
                    rd(F, [(s, LO, ranks(c)), (s, HI, [rk])])
                    continue
                far = [slot((c - 2 * i) % 8, k, d) for i in (1, 2, 3)]
                out = ([slot(c, k, d)] if d == rdie else []) + far
                if BATCH:
                    for s in out:
                        wait_arr(F, "g", s)
                    rd(F, [(s, SPLIT[len(out)][n], [mate]) for n, s in enumerate(out)]
                       + [(s, SPLIT[3][n] << 8, [rk]) for n, s in enumerate(far)])
                    continue
                for s in out:
                    wait_arr(F, "g", s)
                    rd(F, [(s, LO, [mate])] + ([(s, HI, [rk])] if s in far else []))
    for c in range(8):
        rk = roles(c)[0]
        plan = {"sync": [((c - 2 * i) % 8, k) for k in range(C) for i in (1, 2, 3)],
                "scalar": [(((c ^ 1) - 2 * i) % 8, k) for k in range(C) for i in (1, 2, 3)],
                "g": [(c ^ 1, k) for k in range(C)]}
        for name in ("g", "sync", "scalar"):
            for src, k in plan[name]:
                s = slot(src, k, 0)
                wait_arr(rk, name, s)
                wait_arr(rk, name, s + 1)
                qu(rk, name).append(("st", s, s + 2, "st_" + name))
            qu(rk, name).append(("wait", "st_" + name, 16 * len(plan[name])))
        qu(rk, "g").append(("wait", "own", 16))
    for core in sent:
        qu(core, "g").append(("wait", "sent", sent[core]))
    return ops


PLAN = build()
SCRATCH = dict(("L%d" % k, ("dram", [16, 128, 8 * ROWS[k]], "float32")) for k in range(C))
SEMAPHORES = ["sent", "own", "st_g", "st_sync", "st_scalar"] + ["a%d" % i for i in range(16 * C)]


def rank_program(g, core, T, topo):
    prog = PLAN.get(core)
    if prog is None:
        return
    for name, q in (("g", g), ("sync", g.sync), ("scalar", g.scalar)):
        for o in prog[name]:
            if o[0] == "wait":
                q.wait_ge(T.sem[o[1]], o[2])
            elif o[0] == "ld" or o[0] == "st":
                k, a, b = o[1] // 16, o[1] % 16, o[1] % 16 + o[2] - o[1]
                j = a // 2
                r0 = BASE[k] + (a % 2) * ROWS[k]
                r1 = r0 + (b - a) * ROWS[k]
                if o[0] == "ld":
                    q.dma_start(T["L%d" % k][a:b], T.x[r0:r1, :]).then_inc(T.sem[o[3]], 16)
                else:
                    q.dma_start(T.y[r0:r1, 1024 * j:1024 * (j + 1)], T["L%d" % k][a:b]).then_inc(T.sem[o[3]], 16)
            elif o[0] == "own":
                q.dma_start(T.y[:, 1024 * o[1]:1024 * (o[1] + 1)], T.x[:, :]).then_inc(T.sem[o[2]], 16)
            else:
                trs = []
                for s, m, dsts in o[1]:
                    ap = T["L%d" % (s // 16)][s % 16]
                    ids = [DstId(rid=topo.addr(d)[0], pnc=topo.addr(d)[1]) for d in dsts]
                    trs.append(RemoteDMATransfer(dst_ids=ids, dma_engine_mask=m, remote_sem=T.sem["a%d" % s],
                                                 srcs=[ap], dsts=[ap for d in dsts]))
                q.remote_dma_fused(trs, local_sem=T.sem.sent)
